import numpy as np
import ml_dtypes


def mxq(x, axis, fmt="e4m3"):
    dtype, down = {"e4m3": (ml_dtypes.float8_e4m3fn, 7), "e5m2": (ml_dtypes.float8_e5m2, 14)}[fmt]
    v = np.moveaxis(np.asarray(x, np.float32).astype(ml_dtypes.bfloat16).astype(np.float64), axis, -1)
    blocks = v.reshape(v.shape[:-1] + (-1, 32))
    amax = np.abs(blocks).max(-1, keepdims=True)
    byte = np.maximum(np.where(amax > 0, np.frexp(amax)[1] - 1 + 127, 0) - down, 1)
    scale = np.exp2(byte - 127.0)
    codes = (blocks / scale).astype(np.float32).astype(dtype).astype(np.float64)
    return np.moveaxis((codes * scale).reshape(v.shape), -1, axis)


WIDE = False


def mx_kscale(k):
    if not WIDE:
        return np.ones(k)
    levels = np.array([10, -10, 5, -5, 0])
    if k % 512:
        return np.exp2(np.random.permutation(np.resize(levels, k // 32))).repeat(32)
    a = np.empty((k // 512, 16))
    for p in range(k // 512):
        a[p, :8] = np.random.permutation(np.resize(levels, 8))
        for g in range(8):
            far = levels[np.abs(levels - a[p, g]) >= 10]
            a[p, g + 8] = far[np.random.randint(len(far))]
    return np.exp2(a.ravel()).repeat(32)


def f64(x):
    return np.asarray(x).astype(np.float64)


def striped(idx):
    return np.tile(idx.reshape(-1, 16).T, (8, 1)).astype(np.uint16)


def unstriped(offs):
    return offs[:16].T.reshape(-1).astype(np.int64)


def relu(v):
    return np.maximum(v, 0.0)


K, T, S, V, H, N = 1024, 2048, 768, 384, 512, 256


def setup_inputs():
    n = np.random.standard_normal
    s = mx_kscale(K)[:, None]
    u = mx_kscale(H)
    return {
        "xT": (n((K, T)) * s).astype(np.float32),
        "w1": (n((K, H)) / np.sqrt(K) / s * u).astype(np.float32),
        "w2": (n((H, N)) / np.sqrt(2 * H) / u[:, None]).astype(np.float32),
        "w3": (n((H, N)) / np.sqrt(2 * H) / u[:, None]).astype(np.float32),
        "offs": striped(np.random.permutation(T)[:S]),
    }


def reference(xT, w1, w2, w3, offs):
    xq = mxq(f64(xT)[:, unstriped(offs)], 0, "e4m3")
    h = relu(mxq(f64(w1), 0, "e4m3").T @ xq)
    low = 0.5 * (h[:, :V] + h[:, V:2 * V])
    high = 0.5 * (h[:, :V] - h[:, V:2 * V])
    return mxq(f64(w2), 0, "e4m3").T @ mxq(low, 0, "e4m3") + mxq(f64(w3), 0, "e4m3").T @ mxq(high, 0, "e4m3")

from contextlib import ExitStack

import concourse.mybir as mybir

K, T, S, V, H, N = 1024, 2048, 768, 384, 512, 256
FLOPS = 2 * K * H * S + 2 * 2 * H * N * V

F32 = mybir.dt.float32
BF16 = mybir.dt.bfloat16
U32 = mybir.dt.uint32
U16 = mybir.dt.uint16
U8 = mybir.dt.uint8
FP8X4 = mybir.dt.float8_e4m3fn_x4
ALU = mybir.AluOpType
ACT = mybir.ActivationFunctionType

P = 128
PACK = 4
K_PASS = P * PACK
PASSES = K // K_PASS
BLK = 128
BLOCKS = V // BLK
HALF = H // 2


def quantize(nc, codes, scales, values):
    nc.vector.quantize_mx(out=codes.bitcast(FP8X4), scales=scales, in_=values)


def tile_picked_haar_relu_e_kernel(tc, xT, w1, w2, w3, offs, out):
    nc = tc.nc
    with ExitStack() as ctx:
        keep = ctx.enter_context(tc.tile_pool(name="keep", bufs=1))
        psum = ctx.enter_context(tc.psum_pool(name="psum", bufs=1))

        offsets = keep.tile([P, S // 16], U16, name="offsets")
        nc.sync.dma_start(offsets[:], offs)

        x_rows = xT.rearrange("(g p j) c -> g j p c", g=PASSES, j=PACK)
        planes = {}
        for g in range(PASSES):
            for j in range(PACK):
                planes[g, j] = keep.tile([P, T], F32, name="plane%d%d" % (g, j))
                nc.sync.dma_start(planes[g, j][:], x_rows[g, j])
        w1_rows = w1.rearrange("(g p j) c -> g p j c", g=PASSES, j=PACK)
        w1_raw = {}
        for g in range(PASSES):
            for h in range(2):
                w1_raw[g, h] = keep.tile([P, PACK, HALF], F32, name="w1raw%d%d" % (g, h))
                nc.sync.dma_start(w1_raw[g, h][:], w1_rows[g, :, :, h * HALF:(h + 1) * HALF])
        w23_raw = []
        for b, w in enumerate((w2, w3)):
            raw = keep.tile([P, PACK, N], F32, name="w23raw%d" % b)
            nc.sync.dma_start(raw[:], w.rearrange("(p j) n -> p j n", j=PACK))
            w23_raw.append(raw)

        x_codes = [keep.tile([P, S], U32, name="xcodes%d" % g, align_bytes=64) for g in range(PASSES)]
        x_scales = [keep.tile([P, S], U8, name="xscales%d" % g, align_bytes=64) for g in range(PASSES)]
        for g in range(PASSES):
            flat_planes = PACK if g == 0 else 2
            flat = keep.tile([P, flat_planes, S], BF16, name="flat%d" % g, align_bytes=64)
            woven = keep.tile([P, S, PACK], BF16, name="woven%d" % g, align_bytes=64)
            for j in range(flat_planes):
                nc.vector.tensor_copy(flat[:, j, :], planes[g, j][:].indirect(offsets[:]))
            nc.scalar.activation(woven[:, :, 0:flat_planes], flat[:].rearrange("p j n -> p n j"), ACT.Copy)
            for j in range(flat_planes, PACK):
                nc.vector.tensor_copy(woven[:, :, j], planes[g, j][:].indirect(offsets[:]))
            values = woven[:].rearrange("p n j -> p (n j)")
            for lo, hi in ((0, 512), (512, S)):
                quantize(nc, x_codes[g][:, lo:hi], x_scales[g][:, lo:hi], values[:, PACK * lo:PACK * hi])

        w1_codes = [keep.tile([P, H], U32, name="w1codes%d" % g, align_bytes=64) for g in range(PASSES)]
        w1_scales = [keep.tile([P, H], U8, name="w1scales%d" % g, align_bytes=64) for g in range(PASSES)]
        M_HALF = P // 2
        for g in range(PASSES):
            for h in range(2):
                dealt = keep.tile([P, PACK, M_HALF, PACK], BF16, name="w1dealt%d%d" % (g, h), align_bytes=64)
                src = w1_raw[g, h][:].rearrange("p j (m t) -> p m j t", t=PACK)
                dst = dealt[:].rearrange("p t m j -> p m j t")
                if (g, h) == (PASSES - 1, 1):
                    nc.vector.tensor_copy(dst, src)
                else:
                    nc.scalar.copy(dst, src)
                for t in range(PACK):
                    cols = slice(t * P + h * M_HALF, t * P + (h + 1) * M_HALF)
                    quantize(nc, w1_codes[g][:, cols], w1_scales[g][:, cols],
                             dealt[:, t].rearrange("p m j -> p (m j)"))

        w23_codes, w23_scales = [], []
        w23_woven = []
        for b in range(2):
            w23_woven.append(keep.tile([P, N, PACK], BF16, name="w23woven%d" % b, align_bytes=64))
            w23_codes.append(keep.tile([P, N], U32, name="w23codes%d" % b, align_bytes=64))
            w23_scales.append(keep.tile([P, N], U8, name="w23scales%d" % b, align_bytes=64))

        def prepare_w23(b):
            for mt in range(2):
                cols = slice(mt * P, (mt + 1) * P)
                nc.scalar.copy(w23_woven[b][:, cols, :], w23_raw[b][:, :, cols].rearrange("p j n -> p n j"))
            quantize(nc, w23_codes[b][:], w23_scales[b][:], w23_woven[b][:].rearrange("p n j -> p (n j)"))

        def first_product(name, col0):
            bank = psum.tile([P, PACK, BLK], F32, name=name)
            cols = slice(col0, col0 + BLK)
            for t in range(PACK):
                m = slice(t * P, (t + 1) * P)
                for g in range(PASSES):
                    nc.tensor.matmul_mx(
                        out=bank[:, t, :],
                        lhsT=w1_codes[g][:, m].bitcast(FP8X4), lhsT_scale=w1_scales[g][:, m],
                        rhs=x_codes[g][:, cols].bitcast(FP8X4), rhs_scale=x_scales[g][:, cols],
                        start=(g == 0), stop=(g == PASSES - 1))
            return bank

        bands = []

        def haar(i):
            second = first_product("second%d" % i, V + i * BLK)
            first = first_product("first%d" % i, i * BLK)
            relu2 = keep.tile([P, BLK, PACK], F32, name="relu%d" % i)
            nc.scalar.activation(relu2[:], second[:].rearrange("p t n -> p n t"), ACT.Relu)
            band = keep.tile([P, 2, BLK, PACK], BF16, name="band%d" % i, align_bytes=64)
            for b, op in enumerate((ALU.add, ALU.subtract)):
                nc.vector.scalar_tensor_tensor(
                    band[:, b], first[:].rearrange("p t n -> p n t"), 0.0, relu2[:], ALU.max, op)
            bands.append(band)

        def second_product(i):
            codes = keep.tile([P, 2 * BLK], U32, name="bandcodes%d" % i, align_bytes=64)
            scales = keep.tile([P, 2 * BLK], U8, name="bandscales%d" % i, align_bytes=64)
            quantize(nc, codes[:], scales[:], bands[i][:].rearrange("p b n t -> p (b n t)"))
            acc = psum.tile([P, 2, BLK], F32, name="acc%d" % (i % 2))
            for mt in range(2):
                m = slice(mt * P, (mt + 1) * P)
                for b in range(2):
                    cols = slice(b * BLK, (b + 1) * BLK)
                    nc.tensor.matmul_mx(
                        out=acc[:, mt, :],
                        lhsT=w23_codes[b][:, m].bitcast(FP8X4), lhsT_scale=w23_scales[b][:, m],
                        rhs=codes[:, cols].bitcast(FP8X4), rhs_scale=scales[:, cols],
                        start=(b == 0), stop=(b == 1))
            res = keep.tile([P, 2, BLK], F32, name="res%d" % i)
            nc.scalar.activation(res[:], acc[:], ACT.Copy, scale=0.5)
            nc.sync.dma_start(
                out.rearrange("(mt p) v -> p mt v", p=P)[:, :, i * BLK:(i + 1) * BLK], res[:])

        prepare_w23(0)
        haar(0)
        prepare_w23(1)
        for i in range(1, BLOCKS):
            haar(i)
            second_product(i - 1)
        second_product(BLOCKS - 1)
